import numpy as np
import ml_dtypes


def mxq(x, axis, fmt="e4m3"):
    dtype, down = {"e4m3": (ml_dtypes.float8_e4m3fn, 7), "e5m2": (ml_dtypes.float8_e5m2, 14)}[fmt]
    v = np.moveaxis(np.asarray(x, np.float32).astype(ml_dtypes.bfloat16).astype(np.float64), axis, -1)
    blocks = v.reshape(v.shape[:-1] + (-1, 32))
    amax = np.abs(blocks).max(-1, keepdims=True)
    byte = np.maximum(np.where(amax > 0, np.frexp(amax)[1] - 1 + 127, 0) - down, 1)
    scale = np.exp2(byte - 127.0)
    codes = (blocks / scale).astype(np.float32).astype(dtype).astype(np.float64)
    return np.moveaxis((codes * scale).reshape(v.shape), -1, axis)


WIDE = False


def mx_kscale(k):
    if not WIDE:
        return np.ones(k)
    levels = np.array([10, -10, 5, -5, 0])
    if k % 512:
        return np.exp2(np.random.permutation(np.resize(levels, k // 32))).repeat(32)
    a = np.empty((k // 512, 16))
    for p in range(k // 512):
        a[p, :8] = np.random.permutation(np.resize(levels, 8))
        for g in range(8):
            far = levels[np.abs(levels - a[p, g]) >= 10]
            a[p, g + 8] = far[np.random.randint(len(far))]
    return np.exp2(a.ravel()).repeat(32)


def f64(x):
    return np.asarray(x).astype(np.float64)


def striped(idx):
    return np.tile(idx.reshape(-1, 16).T, (8, 1)).astype(np.uint16)


def unstriped(offs):
    return offs[:16].T.reshape(-1).astype(np.int64)


def striped8(idx):
    return np.concatenate([x.reshape(-1, 16).T for x in idx]).astype(np.uint16)


def runs(offs, k):
    lists = np.stack([offs[16 * r : 16 * r + 16].T.reshape(-1) for r in range(8)]).astype(np.int64)
    return lists[np.arange(k) % 512 // 64]


def pack_weight(w):
    k, n = w.shape
    w = f64(np.asarray(w, np.float32).astype(ml_dtypes.bfloat16)).reshape(k // 32, 32, n)
    amax = np.abs(w).max(1)
    byte = np.clip(np.where(amax > 0, np.frexp(amax)[1] - 1 + 127 - 7, 1), 1, 254)
    scaled = (w * np.exp2(127.0 - byte)[:, None, :]).reshape(k, n).astype(np.float32)
    words = np.ascontiguousarray(scaled.reshape(k // 512, 128, 4, n).transpose(0, 1, 3, 2)).astype(ml_dtypes.float8_e4m3fn).view(np.uint8)
    return words, np.ascontiguousarray(byte.astype(np.uint8).reshape(k // 512, 16, n))


def unpack_weight(words, scales):
    g, p, n, _ = words.shape
    vals = np.ascontiguousarray(words).view(ml_dtypes.float8_e4m3fn).astype(np.float64) * np.repeat(np.exp2(scales.astype(np.float64) - 127.0), 8, axis=1)[..., None]
    return vals.transpose(0, 1, 3, 2).reshape(g * 512, n)


K, T, S, N, G, H, W = 512, 1024, 512, 512, 2048, 512, 384


def setup_inputs():
    n = np.random.standard_normal
    s = mx_kscale(K)[:, None]
    u = mx_kscale(S)
    packed_xT = pack_weight(n((K, T)) * s)
    packed_dT = pack_weight(n((K, G)) / s)
    return {
        "x_words": packed_xT[0],
        "x_scales": packed_xT[1],
        "d_words": packed_dT[0],
        "d_scales": packed_dT[1],
        "gn": (np.random.uniform(0.5, 1.5, (H, 1)) * u[:, None]).astype(np.float32),
        "w1": (n((H, N)) / np.sqrt(2 * H) / u[:, None]).astype(np.float32),
        "w2": (n((K, N)) / np.sqrt(2 * K) / s).astype(np.float32),
        "offs": striped(np.random.permutation(T)[:S]),
        "k1": striped8(np.random.randint(0, G, (8, H))),
        "n1": striped(np.random.permutation(S)[:W]),
        "n2": striped(np.random.permutation(S)[:W]),
        "two": striped(np.random.permutation(T)[:S]),
        "n3": striped8(np.stack([np.random.permutation(S) for _ in range(8)])),
        "n4": striped8(np.stack([np.random.permutation(S) for _ in range(8)])),
    }


def reference(x_words, x_scales, d_words, d_scales, gn, w1, w2, offs, k1, n1, n2, two, n3, n4):
    d_k1 = unpack_weight(d_words, d_scales)[np.arange(K)[:, None], runs(k1, K)]
    xq = unpack_weight(x_words, x_scales)[:, unstriped(offs)]
    h = 0.0625 * (d_k1.T @ xq)
    pa = h[:, unstriped(n2)]
    old = h[:, unstriped(n1)]
    ra = np.minimum(pa, old) - (0.5 * pa)
    ds = h.copy()
    ds[:, unstriped(n1)] = ra
    z = f64(gn) * ds
    x_two = unpack_weight(x_words, x_scales)[:, unstriped(two)]
    h2 = mxq(f64(w1), 0, "e4m3").T @ mxq(z, 0, "e4m3") + mxq(f64(w2), 0, "e4m3").T @ x_two
    return (h2[np.arange(N)[:, None], runs(n3, N)]) / (np.abs(h2) + np.abs(h2[np.arange(N)[:, None], runs(n4, N)]) + 0.5)

@@ -1,0 +1,218 @@
+from contextlib import ExitStack
+
+import concourse.mybir as mybir
+
+K, T, S, N, G, H, W = 512, 1024, 512, 512, 2048, 512, 384
+FLOPS = 2 * K * H * S + 2 * H * N * S + 2 * K * N * S
+
+F32 = mybir.dt.float32
+BF16 = mybir.dt.bfloat16
+I32 = mybir.dt.int32
+U32 = mybir.dt.uint32
+U16 = mybir.dt.uint16
+U8 = mybir.dt.uint8
+FP8X4 = mybir.dt.float8_e4m3fn_x4
+ALU = mybir.AluOpType
+ACT = mybir.ActivationFunctionType
+
+P = 128
+PACK = 4
+HALF = S // 2
+W2_EARLY = 256
+
+
+def tile_picked_pqmixkminnorm2_none_p_kernel(
+    tc, x_words, x_scales, d_words, d_scales, gn, w1, w2, offs, k1, n1, n2, two, n3, n4, out
+):
+    nc = tc.nc
+    with ExitStack() as ctx:
+        keep = ctx.enter_context(tc.tile_pool(name="keep", bufs=1))
+        shared = ctx.enter_context(tc.tile_pool(name="shared", bufs=1))
+        psum = ctx.enter_context(tc.psum_pool(name="psum", bufs=1))
+
+        def sb(name, shape, dtype, tag=None):
+            return keep.tile(shape, dtype, name=name, tag=tag or name, align_bytes=64)
+
+        def load_list(name, src):
+            tile = sb(name, list(src.shape), U16)
+            nc.sync.dma_start(tile[:], src)
+            return tile
+
+        x_scale_table = sb("x_scale_table", [P, T], U8)
+        d_scale_table = sb("d_scale_table", [P, G], U8)
+        x_word_table = sb("x_word_table", [P, T], I32)
+        d_word_table = sb("d_word_table", [P, G], I32, tag="dictionary_then_w1")
+        d_plane = sb("d_plane", [P, H], U8)
+        nc.vector.memset(x_scale_table[:].bitcast(I32), 0)
+        nc.vector.memset(d_scale_table[:].bitcast(I32), 0)
+        nc.vector.memset(d_plane[:].bitcast(I32), 0)
+
+        w2_rows = w2.rearrange("(p j) m -> p j m", j=PACK)
+        k1_list = load_list("k1_list", k1)
+        offs_list = load_list("offs_list", offs)
+        nc.sync.dma_start(d_scale_table[::8, :].bitcast(I32), d_scales[0].bitcast(I32))
+        for j in range(4):
+            nc.sync.dma_start(x_scale_table[j::32, :].bitcast(I32), x_scales[0, j::4, :].bitcast(I32))
+        nc.sync.dma_start(x_word_table[:], x_words[0].rearrange("p n r -> p (n r)").bitcast(I32))
+        nc.sync.dma_start(d_word_table[:], d_words[0].rearrange("p n r -> p (n r)").bitcast(I32))
+        two_list = load_list("two_list", two)
+        n2_list = load_list("n2_list", n2)
+        n1_list = load_list("n1_list", n1)
+        n4_list = load_list("n4_list", n4)
+        n3_list = load_list("n3_list", n3)
+        gain = sb("gain", [P, PACK], F32)
+        nc.gpsimd.dma_start(gain[:], gn.rearrange("(p t) o -> p (t o)", t=PACK))
+
+        d_bytes = shared.tile([P, H], U8, name="d_bytes", offset=8192 - 256, align_bytes=64)
+        nc.vector.tensor_copy(d_bytes[:], d_scale_table[:].indirect(k1_list[:]))
+        d_bytes_dealt = sb("d_bytes_dealt", [P, H], U8)
+        nc.vector.tensor_copy(
+            d_bytes_dealt[:].rearrange("p (t m) -> p m t", t=PACK),
+            d_bytes[:].rearrange("p (m t) -> p m t", t=PACK),
+        )
+        w2_early = shared.tile([P, PACK, W2_EARLY], F32, name="w2_early", offset=4096, align_bytes=64)
+        w2_late = shared.tile([P, PACK, W2_EARLY], F32, name="w2_late", offset=8192, align_bytes=64)
+        nc.scalar.dma_start(w2_early[:], w2_rows[:, :, :W2_EARLY])
+        nc.scalar.dma_start(w2_late[:], w2_rows[:, :, W2_EARLY:])
+        for j in range(4):
+            nc.scalar.dma_start(d_plane[j::32, :].bitcast(I32), d_bytes_dealt[8 * j :: 32, :].bitcast(I32))
+
+        xq_plane = sb("xq_plane", [P, S], U8)
+        nc.vector.tensor_copy(xq_plane[:], x_scale_table[:].indirect(offs_list[:]))
+        xq_words = sb("xq_words", [P, S], U32)
+        nc.vector.tensor_copy(xq_words[:], x_word_table[:].bitcast(U32).indirect(offs_list[:]))
+        d_picked = shared.tile([P, H], U32, name="d_picked", offset=0, align_bytes=64)
+        nc.vector.tensor_copy(d_picked[:], d_word_table[:].bitcast(U32).indirect(k1_list[:]))
+        d_dealt = sb("d_dealt", [P, H], U32)
+        nc.vector.tensor_copy(
+            d_dealt[:].bitcast(I32).rearrange("p (t m) -> p m t", t=PACK),
+            d_picked[:].bitcast(I32).rearrange("p (m t) -> p m t", t=PACK),
+        )
+        w1_raw = sb("w1_raw", [P, PACK, N], F32, tag="dictionary_then_w1")
+        nc.sync.dma_start(w1_raw[:], w1.rearrange("(p j) m -> p j m", j=PACK))
+
+        def round_columns(copy, grouped, first, raw):
+            width = raw.shape[2]
+            copy(
+                grouped[:].rearrange("p (t m j) -> p m j t", t=PACK, j=PACK)[:, first // PACK : (first + width) // PACK],
+                raw.rearrange("p j (m t) -> p m j t", t=PACK),
+            )
+
+        def quantise(name, grouped):
+            words = sb(name + "_words", [P, N], U32)
+            plane = sb(name + "_plane", [P, N], U8)
+            nc.vector.quantize_mx(out=words[:].bitcast(FP8X4), scales=plane[:], in_=grouped[:])
+            return words, plane
+
+        w2_grouped = sb("w2_grouped", [P, PACK * N], BF16)
+        round_columns(nc.scalar.copy, w2_grouped, 0, w2_early[:])
+        round_columns(nc.scalar.copy, w2_grouped, W2_EARLY, w2_late[:])
+
+        h_banks = []
+        for t in range(PACK):
+            cols = slice(t * P, (t + 1) * P)
+            bank = psum.tile([P, S], F32, name=f"h_bank{t}")
+            nc.tensor.matmul_mx(
+                out=bank[:], lhsT=d_dealt[:, cols].bitcast(FP8X4), lhsT_scale=d_plane[:, cols],
+                rhs=xq_words[:].bitcast(FP8X4), rhs_scale=xq_plane[:], start=True, stop=True,
+            )
+            h_banks.append(bank)
+
+        ds = [sb(f"ds{t}", [P, S], F32) for t in range(PACK)]
+        minus_half_pa = [sb(f"minus_half_pa{t}", [P, W], F32) for t in range(PACK)]
+        old_less = [sb(f"old_less{t}", [P, W], F32) for t in range(PACK)]
+        ra = [sb(f"ra{t}", [P, W], F32) for t in range(PACK)]
+        for t in range(PACK):
+            if t in (3,):
+                nc.vector.tensor_scalar(ds[t][:], h_banks[t][:], 0.0625, None, ALU.mult)
+            else:
+                nc.scalar.activation(ds[t][:], h_banks[t][:], ACT.Copy, scale=0.0625)
+        for t in range(PACK):
+            nc.scalar.activation(minus_half_pa[t][:], ds[t][:].indirect(n2_list[:]), ACT.Copy, scale=-0.5)
+        for t in range(PACK):
+            nc.vector.tensor_tensor(old_less[t][:], ds[t][:].indirect(n1_list[:]), minus_half_pa[t][:], ALU.add)
+            nc.vector.scalar_tensor_tensor(ra[t][:], minus_half_pa[t][:], -1.0, old_less[t][:], ALU.mult, ALU.min)
+        for t in range(PACK):
+            if t in (3,):
+                nc.vector.tensor_copy(ds[t][:].indirect(n1_list[:]), ra[t][:])
+            else:
+                nc.scalar.activation(ds[t][:].indirect(n1_list[:]), ra[t][:], ACT.Copy)
+
+        xt_words = shared.tile([P, S], U32, name="xt_words", offset=S, align_bytes=64)
+        nc.vector.tensor_copy(xt_words[:], x_word_table[:].bitcast(U32).indirect(two_list[:]))
+        xt_plane = shared.tile([P, S], U8, name="xt_plane", offset=0, align_bytes=64)
+        nc.vector.tensor_copy(xt_plane[:], x_scale_table[:].indirect(two_list[:]))
+
+        w2_words, w2_plane = quantise("w2", w2_grouped)
+        w1_grouped = sb("w1_grouped", [P, PACK * N], BF16, tag="rounded")
+        for c in range(2):
+            round_columns(nc.vector.tensor_copy, w1_grouped, c * N // 2, w1_raw[:, :, c * N // 2 : (c + 1) * N // 2])
+        w1_words, w1_plane = quantise("w1", w1_grouped)
+
+        h2_banks = []
+        for t in range(PACK):
+            cols = slice(t * P, (t + 1) * P)
+            bank = psum.tile([P, S], F32, name=f"h2_bank{t}")
+            nc.tensor.matmul_mx(
+                out=bank[:], lhsT=w2_words[:, cols].bitcast(FP8X4), lhsT_scale=w2_plane[:, cols],
+                rhs=xt_words[:].bitcast(FP8X4), rhs_scale=xt_plane[:], start=True, stop=False,
+            )
+            h2_banks.append(bank)
+
+        z_pairs = sb("z_pairs", [P, 2, S, 2], BF16, tag="rounded")
+        for t in (0, 3, 1):
+            nc.vector.tensor_scalar(z_pairs[:, t // 2, :, t % 2], ds[t][:], gain[:, t : t + 1], None, ALU.mult)
+        for c in range(2):
+            cols = slice(c * HALF, (c + 1) * HALF)
+            t = 2
+            nc.vector.tensor_scalar(z_pairs[:, t // 2, cols, t % 2], ds[t][:, cols], gain[:, t : t + 1], None, ALU.mult)
+        z_grouped = sb("z_grouped", [P, PACK * S], BF16)
+        z_words = sb("z_words", [P, S], U32)
+        z_plane = sb("z_plane", [P, S], U8)
+        pair_words = z_pairs[:].rearrange("p u j e -> p u (j e)").bitcast(F32)
+        for c in range(2):
+            cols = slice(c * HALF, (c + 1) * HALF)
+            nc.vector.tensor_copy(
+                z_grouped[:].bitcast(F32).rearrange("p (j u) -> p j u", u=2)[:, cols, :],
+                pair_words.rearrange("p u j -> p j u")[:, cols, :],
+            )
+        for c in range(2):
+            cols = slice(c * HALF, (c + 1) * HALF)
+            nc.vector.quantize_mx(
+                out=z_words[:, cols].bitcast(FP8X4), scales=z_plane[:, cols],
+                in_=z_grouped[:, PACK * c * HALF : PACK * (c + 1) * HALF],
+            )
+        for t in range(PACK):
+            cols = slice(t * P, (t + 1) * P)
+            nc.tensor.matmul_mx(
+                out=h2_banks[t][:], lhsT=w1_words[:, cols].bitcast(FP8X4), lhsT_scale=w1_plane[:, cols],
+                rhs=z_words[:].bitcast(FP8X4), rhs_scale=z_plane[:], start=False, stop=True,
+            )
+
+        out_rows = out.rearrange("(p t) j -> t p j", t=PACK)
+        value_window = [sb(f"value_window{t}", [P, 2 * S], F32) for t in range(PACK)]
+        size_window = [sb(f"size_window{t}", [P, 2 * S], F32) for t in range(PACK)]
+        den = [sb(f"den{t}", [P, S], F32) for t in range(PACK)]
+        for t in range(PACK):
+            nc.gpsimd.memset(size_window[t][:, S:], 0.0)
+            nc.scalar.activation(size_window[t][:, :S], h2_banks[t][:], ACT.Abs)
+        for t in (3,):
+            nc.scalar.activation(value_window[t][:, S:], h2_banks[t][:], ACT.Abs)
+        for t in range(PACK + 1):
+            if t < PACK and t not in (3,):
+                nc.vector.tensor_copy(value_window[t][:, S:], size_window[t][:, :S])
+            if t > 0:
+                nc.vector.tensor_tensor(den[t - 1][:], size_window[t - 1][:].indirect(n4_list[:]), value_window[t - 1][:, S:], ALU.add)
+        for t in range(PACK):
+            nc.scalar.copy(value_window[t][:, :S], h2_banks[t][:])
+            root = sb(f"root{t}", [P, S], F32)
+            nc.scalar.activation(root[:], den[t][:], ACT.Abs_reciprocal_sqrt, bias=0.5)
+            inverse = sb(f"inverse{t}", [P, S], F32)
+            nc.scalar.activation(inverse[:], root[:], ACT.Square)
+            pieces = 2 if t == PACK - 1 else 1
+            for c in range(pieces):
+                cols = slice(c * S // pieces, (c + 1) * S // pieces)
+                entries = slice(c * S // pieces // 16, (c + 1) * S // pieces // 16)
+                result = sb(f"result{t}_{c}", [P, S // pieces], F32)
+                nc.vector.tensor_tensor(result[:], value_window[t][:].indirect(n3_list[:, entries]), inverse[:, cols], ALU.mult)
+                nc.sync.dma_start(out_rows[t][:, cols], result[:])

@@ -44,16 +44,18 @@ def tile_picked_pqmixkminnorm2_none_p_kernel(
         d_word_table = sb("d_word_table", [P, G], I32, tag="dictionary_then_w1")
         d_plane = sb("d_plane", [P, H], U8)
         nc.vector.memset(x_scale_table[:].bitcast(I32), 0)
-        nc.vector.memset(d_scale_table[:].bitcast(I32), 0)
         nc.vector.memset(d_plane[:].bitcast(I32), 0)
 
         w2_rows = w2.rearrange("(p j) m -> p j m", j=PACK)
         k1_list = load_list("k1_list", k1)
+        nc.sync.dma_start(
+            d_scale_table[:].bitcast(I32),
+            d_scales[0].bitcast(I32).unsqueeze(1).to_broadcast([16, 8, G // 4]),
+        )
         offs_list = load_list("offs_list", offs)
-        nc.sync.dma_start(d_scale_table[::8, :].bitcast(I32), d_scales[0].bitcast(I32))
+        nc.sync.dma_start(x_word_table[:], x_words[0].rearrange("p n r -> p (n r)").bitcast(I32))
         for j in range(4):
             nc.sync.dma_start(x_scale_table[j::32, :].bitcast(I32), x_scales[0, j::4, :].bitcast(I32))
-        nc.sync.dma_start(x_word_table[:], x_words[0].rearrange("p n r -> p (n r)").bitcast(I32))
         nc.sync.dma_start(d_word_table[:], d_words[0].rearrange("p n r -> p (n r)").bitcast(I32))
         two_list = load_list("two_list", two)
         n2_list = load_list("n2_list", n2)
@@ -61,7 +63,7 @@ def tile_picked_pqmixkminnorm2_none_p_kernel(
         n4_list = load_list("n4_list", n4)
         n3_list = load_list("n3_list", n3)
         gain = sb("gain", [P, PACK], F32)
-        nc.gpsimd.dma_start(gain[:], gn.rearrange("(p t) o -> p (t o)", t=PACK))
+        nc.sync.dma_start(gain[:], gn.rearrange("(p t) o -> p (t o)", t=PACK))
 
         d_bytes = shared.tile([P, H], U8, name="d_bytes", offset=8192 - 256, align_bytes=64)
         nc.vector.tensor_copy(d_bytes[:], d_scale_table[:].indirect(k1_list[:]))
@@ -123,11 +125,10 @@ def tile_picked_pqmixkminnorm2_none_p_kernel(
         old_less = [sb(f"old_less{t}", [P, W], F32) for t in range(PACK)]
         ra = [sb(f"ra{t}", [P, W], F32) for t in range(PACK)]
         for t in range(PACK):
-            if t in (3,):
+            if t in ():
                 nc.vector.tensor_scalar(ds[t][:], h_banks[t][:], 0.0625, None, ALU.mult)
             else:
                 nc.scalar.activation(ds[t][:], h_banks[t][:], ACT.Copy, scale=0.0625)
-        for t in range(PACK):
             nc.scalar.activation(minus_half_pa[t][:], ds[t][:].indirect(n2_list[:]), ACT.Copy, scale=-0.5)
         for t in range(PACK):
             nc.vector.tensor_tensor(old_less[t][:], ds[t][:].indirect(n1_list[:]), minus_half_pa[t][:], ALU.add)
@@ -149,15 +150,16 @@ def tile_picked_pqmixkminnorm2_none_p_kernel(
             round_columns(nc.vector.tensor_copy, w1_grouped, c * N // 2, w1_raw[:, :, c * N // 2 : (c + 1) * N // 2])
         w1_words, w1_plane = quantise("w1", w1_grouped)
 
-        h2_banks = []
-        for t in range(PACK):
+        parts = [(0, slice(0, HALF)), (0, slice(HALF, S))] + [(t, slice(0, S)) for t in range(1, PACK)]
+        h2_parts = []
+        for number, (t, places) in enumerate(parts):
             cols = slice(t * P, (t + 1) * P)
-            bank = psum.tile([P, S], F32, name=f"h2_bank{t}")
+            bank = psum.tile([P, places.stop - places.start], F32, name=f"h2_bank{number}", tag="h_bank0" if number == 0 else f"h2_bank{number}")
             nc.tensor.matmul_mx(
                 out=bank[:], lhsT=w2_words[:, cols].bitcast(FP8X4), lhsT_scale=w2_plane[:, cols],
-                rhs=xt_words[:].bitcast(FP8X4), rhs_scale=xt_plane[:], start=True, stop=False,
+                rhs=xt_words[:, places].bitcast(FP8X4), rhs_scale=xt_plane[:, places], start=True, stop=False,
             )
-            h2_banks.append(bank)
+            h2_parts.append((t, places, bank))
 
         z_pairs = sb("z_pairs", [P, 2, S, 2], BF16, tag="rounded")
         for t in (0, 3, 1):
@@ -182,29 +184,32 @@ def tile_picked_pqmixkminnorm2_none_p_kernel(
                 out=z_words[:, cols].bitcast(FP8X4), scales=z_plane[:, cols],
                 in_=z_grouped[:, PACK * c * HALF : PACK * (c + 1) * HALF],
             )
-        for t in range(PACK):
+        for t, places, bank in h2_parts:
             cols = slice(t * P, (t + 1) * P)
             nc.tensor.matmul_mx(
-                out=h2_banks[t][:], lhsT=w1_words[:, cols].bitcast(FP8X4), lhsT_scale=w1_plane[:, cols],
-                rhs=z_words[:].bitcast(FP8X4), rhs_scale=z_plane[:], start=False, stop=True,
+                out=bank[:], lhsT=w1_words[:, cols].bitcast(FP8X4), lhsT_scale=w1_plane[:, cols],
+                rhs=z_words[:, places].bitcast(FP8X4), rhs_scale=z_plane[:, places], start=False, stop=True,
             )
 
         out_rows = out.rearrange("(p t) j -> t p j", t=PACK)
         value_window = [sb(f"value_window{t}", [P, 2 * S], F32) for t in range(PACK)]
         size_window = [sb(f"size_window{t}", [P, 2 * S], F32) for t in range(PACK)]
         den = [sb(f"den{t}", [P, S], F32) for t in range(PACK)]
-        for t in range(PACK):
-            nc.gpsimd.memset(size_window[t][:, S:], 0.0)
-            nc.scalar.activation(size_window[t][:, :S], h2_banks[t][:], ACT.Abs)
-        for t in (3,):
-            nc.scalar.activation(value_window[t][:, S:], h2_banks[t][:], ACT.Abs)
+        for t, places, bank in h2_parts:
+            nc.scalar.activation(size_window[t][:, places], bank[:], ACT.Abs)
+        for t in ():
+            nc.scalar.activation(value_window[t][:, S:], h2_parts[t + 1][2][:], ACT.Abs)
         for t in range(PACK + 1):
-            if t < PACK and t not in (3,):
-                nc.vector.tensor_copy(value_window[t][:, S:], size_window[t][:, :S])
+            if t < PACK and t not in ():
+                for part, places, bank in h2_parts:
+                    if part == t:
+                        nc.vector.tensor_copy(value_window[t][:, S:][:, places], size_window[t][:, places])
             if t > 0:
                 nc.vector.tensor_tensor(den[t - 1][:], size_window[t - 1][:].indirect(n4_list[:]), value_window[t - 1][:, S:], ALU.add)
         for t in range(PACK):
-            nc.scalar.copy(value_window[t][:, :S], h2_banks[t][:])
+            for part, places, bank in h2_parts:
+                if part == t:
+                    nc.scalar.copy(value_window[t][:, places], bank[:])
             root = sb(f"root{t}", [P, S], F32)
             nc.scalar.activation(root[:], den[t][:], ACT.Abs_reciprocal_sqrt, bias=0.5)
             inverse = sb(f"inverse{t}", [P, S], F32)

@@ -45,6 +45,9 @@ def tile_picked_pqmixkminnorm2_none_p_kernel(
         d_plane = sb("d_plane", [P, H], U8)
         nc.vector.memset(x_scale_table[:].bitcast(I32), 0)
         nc.vector.memset(d_plane[:].bitcast(I32), 0)
+        warm = sb("warm", [P, 8], F32)
+        nc.vector.memset(warm[:], 1.0)
+        nc.scalar.activation(warm[:, 0:1], warm[:, 1:2], ACT.Abs_reciprocal_sqrt)
 
         w2_rows = w2.rearrange("(p j) m -> p j m", j=PACK)
         k1_list = load_list("k1_list", k1)

@@ -17,8 +17,23 @@ ACT = mybir.ActivationFunctionType
 
 P = 128
 PACK = 4
-HALF = S // 2
-W2_EARLY = 256
+QUADRANT = 32
+BLOCK_PARTITIONS = 8
+BLOCKS = K // 32
+LIST_ROWS = 16
+HALVES = [slice(0, S // 2), slice(S // 2, S)]
+
+H_COPIED_BY_VECTOR = (2, 3)
+SCATTERED_BY_VECTOR = 3
+SCATTERED_LAST = 2
+NUMERATOR_BY_SCALAR = 3
+STORED_IN_HALVES = (2, 3)
+
+D_PICKED_AT = 0
+XT_PLANE_AT = 0
+XT_WORDS_AT = 512
+W2_HALVES_AT = (4096, 8192)
+D_BYTES_AT = 8192 - 256
 
 
 def tile_picked_pqmixkminnorm2_none_p_kernel(
@@ -33,10 +48,42 @@ def tile_picked_pqmixkminnorm2_none_p_kernel(
         def sb(name, shape, dtype, tag=None):
             return keep.tile(shape, dtype, name=name, tag=tag or name, align_bytes=64)
 
+        def sb_at(name, shape, dtype, offset):
+            return shared.tile(shape, dtype, name=name, offset=offset, align_bytes=64)
+
         def load_list(name, src):
             tile = sb(name, list(src.shape), U16)
             nc.sync.dma_start(tile[:], src)
             return tile
+
+        def deal(dealt, picked):
+            nc.vector.tensor_copy(
+                dealt.rearrange("p (t m) -> p m t", t=PACK), picked.rearrange("p (m t) -> p m t", t=PACK)
+            )
+
+        def round_weight_half(copy, grouped, cols, raw):
+            copy(
+                grouped[:].rearrange("p (t m j) -> p m j t", t=PACK, j=PACK)[:, cols.start // PACK : cols.stop // PACK],
+                raw.rearrange("p j (m t) -> p m j t", t=PACK),
+            )
+
+        def quantise_weight(name, grouped):
+            words = sb(name + "_words", [P, N], U32)
+            plane = sb(name + "_plane", [P, N], U8)
+            nc.vector.quantize_mx(out=words[:].bitcast(FP8X4), scales=plane[:], in_=grouped[:])
+            return words, plane
+
+        def product(bank, t, stationary, moving, places, start, stop):
+            cols = slice(t * P, (t + 1) * P)
+            nc.tensor.matmul_mx(
+                out=bank[:],
+                lhsT=stationary[0][:, cols].bitcast(FP8X4),
+                lhsT_scale=stationary[1][:, cols],
+                rhs=moving[0][:, places].bitcast(FP8X4),
+                rhs_scale=moving[1][:, places],
+                start=start,
+                stop=stop,
+            )
 
         x_scale_table = sb("x_scale_table", [P, T], U8)
         d_scale_table = sb("d_scale_table", [P, G], U8)
@@ -45,20 +92,18 @@ def tile_picked_pqmixkminnorm2_none_p_kernel(
         d_plane = sb("d_plane", [P, H], U8)
         nc.vector.memset(x_scale_table[:].bitcast(I32), 0)
         nc.vector.memset(d_plane[:].bitcast(I32), 0)
-        warm = sb("warm", [P, 8], F32)
-        nc.vector.memset(warm[:], 1.0)
-        nc.scalar.activation(warm[:, 0:1], warm[:, 1:2], ACT.Abs_reciprocal_sqrt)
+        warm_up = sb("warm_up", [P, 8], F32)
+        nc.vector.memset(warm_up[:], 1.0)
 
-        w2_rows = w2.rearrange("(p j) m -> p j m", j=PACK)
         k1_list = load_list("k1_list", k1)
         nc.sync.dma_start(
             d_scale_table[:].bitcast(I32),
-            d_scales[0].bitcast(I32).unsqueeze(1).to_broadcast([16, 8, G // 4]),
+            d_scales[0].bitcast(I32).unsqueeze(1).to_broadcast([BLOCKS, BLOCK_PARTITIONS, G // 4]),
         )
         offs_list = load_list("offs_list", offs)
         nc.sync.dma_start(x_word_table[:], x_words[0].rearrange("p n r -> p (n r)").bitcast(I32))
-        for j in range(4):
-            nc.sync.dma_start(x_scale_table[j::32, :].bitcast(I32), x_scales[0, j::4, :].bitcast(I32))
+        for j in range(PACK):
+            nc.scalar.dma_start(x_scale_table[j::QUADRANT, :].bitcast(I32), x_scales[0, j::PACK, :].bitcast(I32))
         nc.sync.dma_start(d_word_table[:], d_words[0].rearrange("p n r -> p (n r)").bitcast(I32))
         two_list = load_list("two_list", two)
         n2_list = load_list("n2_list", n2)
@@ -68,159 +113,135 @@ def tile_picked_pqmixkminnorm2_none_p_kernel(
         gain = sb("gain", [P, PACK], F32)
         nc.sync.dma_start(gain[:], gn.rearrange("(p t) o -> p (t o)", t=PACK))
 
-        d_bytes = shared.tile([P, H], U8, name="d_bytes", offset=8192 - 256, align_bytes=64)
+        nc.scalar.activation(warm_up[:, 0:1], warm_up[:, 1:2], ACT.Abs_reciprocal_sqrt)
+
+        d_bytes = sb_at("d_bytes", [P, H], U8, D_BYTES_AT)
         nc.vector.tensor_copy(d_bytes[:], d_scale_table[:].indirect(k1_list[:]))
         d_bytes_dealt = sb("d_bytes_dealt", [P, H], U8)
-        nc.vector.tensor_copy(
-            d_bytes_dealt[:].rearrange("p (t m) -> p m t", t=PACK),
-            d_bytes[:].rearrange("p (m t) -> p m t", t=PACK),
-        )
-        w2_early = shared.tile([P, PACK, W2_EARLY], F32, name="w2_early", offset=4096, align_bytes=64)
-        w2_late = shared.tile([P, PACK, W2_EARLY], F32, name="w2_late", offset=8192, align_bytes=64)
-        nc.scalar.dma_start(w2_early[:], w2_rows[:, :, :W2_EARLY])
-        nc.scalar.dma_start(w2_late[:], w2_rows[:, :, W2_EARLY:])
-        for j in range(4):
-            nc.scalar.dma_start(d_plane[j::32, :].bitcast(I32), d_bytes_dealt[8 * j :: 32, :].bitcast(I32))
+        deal(d_bytes_dealt[:], d_bytes[:])
+        w2_rows = w2.rearrange("(p j) m -> p j m", j=PACK)
+        w2_raw = [sb_at(f"w2_raw{c}", [P, PACK, N // 2], F32, W2_HALVES_AT[c]) for c in range(2)]
+        for c, cols in enumerate(HALVES):
+            nc.scalar.dma_start(w2_raw[c][:], w2_rows[:, :, cols])
+        for j in range(PACK):
+            nc.scalar.dma_start(
+                d_plane[j::QUADRANT, :].bitcast(I32),
+                d_bytes_dealt[BLOCK_PARTITIONS * j :: QUADRANT, :].bitcast(I32),
+            )
 
         xq_plane = sb("xq_plane", [P, S], U8)
         nc.vector.tensor_copy(xq_plane[:], x_scale_table[:].indirect(offs_list[:]))
         xq_words = sb("xq_words", [P, S], U32)
         nc.vector.tensor_copy(xq_words[:], x_word_table[:].bitcast(U32).indirect(offs_list[:]))
-        d_picked = shared.tile([P, H], U32, name="d_picked", offset=0, align_bytes=64)
+        d_picked = sb_at("d_picked", [P, H], U32, D_PICKED_AT)
         nc.vector.tensor_copy(d_picked[:], d_word_table[:].bitcast(U32).indirect(k1_list[:]))
         d_dealt = sb("d_dealt", [P, H], U32)
-        nc.vector.tensor_copy(
-            d_dealt[:].bitcast(I32).rearrange("p (t m) -> p m t", t=PACK),
-            d_picked[:].bitcast(I32).rearrange("p (m t) -> p m t", t=PACK),
-        )
+        deal(d_dealt[:].bitcast(I32), d_picked[:].bitcast(I32))
         w1_raw = sb("w1_raw", [P, PACK, N], F32, tag="dictionary_then_w1")
         nc.sync.dma_start(w1_raw[:], w1.rearrange("(p j) m -> p j m", j=PACK))
 
-        def round_columns(copy, grouped, first, raw):
-            width = raw.shape[2]
-            copy(
-                grouped[:].rearrange("p (t m j) -> p m j t", t=PACK, j=PACK)[:, first // PACK : (first + width) // PACK],
-                raw.rearrange("p j (m t) -> p m j t", t=PACK),
-            )
-
-        def quantise(name, grouped):
-            words = sb(name + "_words", [P, N], U32)
-            plane = sb(name + "_plane", [P, N], U8)
-            nc.vector.quantize_mx(out=words[:].bitcast(FP8X4), scales=plane[:], in_=grouped[:])
-            return words, plane
-
         w2_grouped = sb("w2_grouped", [P, PACK * N], BF16)
-        round_columns(nc.scalar.copy, w2_grouped, 0, w2_early[:])
-        round_columns(nc.scalar.copy, w2_grouped, W2_EARLY, w2_late[:])
+        for c, cols in enumerate(HALVES):
+            round_weight_half(nc.scalar.copy, w2_grouped, cols, w2_raw[c][:])
 
-        h_banks = []
+        h_banks = [psum.tile([P, S], F32, name=f"h_bank{t}") for t in range(PACK)]
         for t in range(PACK):
-            cols = slice(t * P, (t + 1) * P)
-            bank = psum.tile([P, S], F32, name=f"h_bank{t}")
-            nc.tensor.matmul_mx(
-                out=bank[:], lhsT=d_dealt[:, cols].bitcast(FP8X4), lhsT_scale=d_plane[:, cols],
-                rhs=xq_words[:].bitcast(FP8X4), rhs_scale=xq_plane[:], start=True, stop=True,
-            )
-            h_banks.append(bank)
+            product(h_banks[t], t, (d_dealt, d_plane), (xq_words, xq_plane), slice(0, S), True, True)
 
-        ds = [sb(f"ds{t}", [P, S], F32) for t in range(PACK)]
+        ds = [sb(f"ds{t}", [P, 2 * S if t == SCATTERED_BY_VECTOR else S], F32) for t in range(PACK)]
         minus_half_pa = [sb(f"minus_half_pa{t}", [P, W], F32) for t in range(PACK)]
-        old_less = [sb(f"old_less{t}", [P, W], F32) for t in range(PACK)]
-        ra = [sb(f"ra{t}", [P, W], F32) for t in range(PACK)]
         for t in range(PACK):
-            if t in ():
-                nc.vector.tensor_scalar(ds[t][:], h_banks[t][:], 0.0625, None, ALU.mult)
+            if t in H_COPIED_BY_VECTOR:
+                nc.vector.tensor_scalar(ds[t][:, :S], h_banks[t][:], 0.0625, None, ALU.mult)
             else:
-                nc.scalar.activation(ds[t][:], h_banks[t][:], ACT.Copy, scale=0.0625)
+                nc.scalar.activation(ds[t][:, :S], h_banks[t][:], ACT.Copy, scale=0.0625)
             nc.scalar.activation(minus_half_pa[t][:], ds[t][:].indirect(n2_list[:]), ACT.Copy, scale=-0.5)
+        smaller = [sb(f"smaller{t}", [P, W], F32) for t in range(PACK)]
         for t in range(PACK):
-            nc.vector.tensor_tensor(old_less[t][:], ds[t][:].indirect(n1_list[:]), minus_half_pa[t][:], ALU.add)
-            nc.vector.scalar_tensor_tensor(ra[t][:], minus_half_pa[t][:], -1.0, old_less[t][:], ALU.mult, ALU.min)
-        for t in range(PACK):
-            if t in (3,):
-                nc.vector.tensor_copy(ds[t][:].indirect(n1_list[:]), ra[t][:])
+            if t == SCATTERED_BY_VECTOR:
+                old = sb("old", [P, W], F32)
+                nc.scalar.activation(old[:], ds[t][:].indirect(n1_list[:]), ACT.Copy)
+                nc.vector.scalar_tensor_tensor(smaller[t][:], minus_half_pa[t][:], -2.0, old[:], ALU.mult, ALU.min)
             else:
-                nc.scalar.activation(ds[t][:].indirect(n1_list[:]), ra[t][:], ACT.Copy)
+                old_less = sb(f"old_less{t}", [P, W], F32)
+                nc.vector.tensor_tensor(old_less[:], ds[t][:].indirect(n1_list[:]), minus_half_pa[t][:], ALU.add)
+                nc.vector.scalar_tensor_tensor(smaller[t][:], minus_half_pa[t][:], -1.0, old_less[:], ALU.mult, ALU.min)
+        for t in range(PACK):
+            if t == SCATTERED_BY_VECTOR:
+                nc.vector.tensor_tensor(ds[t][:].indirect(n1_list[:]), smaller[t][:], minus_half_pa[t][:], ALU.add)
+            else:
+                nc.scalar.activation(ds[t][:].indirect(n1_list[:]), smaller[t][:], ACT.Copy)
 
-        xt_words = shared.tile([P, S], U32, name="xt_words", offset=S, align_bytes=64)
+        xt_words = sb_at("xt_words", [P, S], U32, XT_WORDS_AT)
         nc.vector.tensor_copy(xt_words[:], x_word_table[:].bitcast(U32).indirect(two_list[:]))
-        xt_plane = shared.tile([P, S], U8, name="xt_plane", offset=0, align_bytes=64)
+        xt_plane = sb_at("xt_plane", [P, S], U8, XT_PLANE_AT)
         nc.vector.tensor_copy(xt_plane[:], x_scale_table[:].indirect(two_list[:]))
 
-        w2_words, w2_plane = quantise("w2", w2_grouped)
-        w1_grouped = sb("w1_grouped", [P, PACK * N], BF16, tag="rounded")
-        for c in range(2):
-            round_columns(nc.vector.tensor_copy, w1_grouped, c * N // 2, w1_raw[:, :, c * N // 2 : (c + 1) * N // 2])
-        w1_words, w1_plane = quantise("w1", w1_grouped)
+        w2_mx = quantise_weight("w2", w2_grouped)
+        w1_grouped = sb("w1_grouped", [P, PACK * N], BF16)
+        for cols in HALVES:
+            round_weight_half(nc.vector.tensor_copy, w1_grouped, cols, w1_raw[:, :, cols])
+        w1_mx = quantise_weight("w1", w1_grouped)
 
-        parts = [(0, slice(0, HALF)), (0, slice(HALF, S))] + [(t, slice(0, S)) for t in range(1, PACK)]
+        parts = [(0, places) for places in HALVES] + [(t, slice(0, S)) for t in range(1, PACK)]
         h2_parts = []
         for number, (t, places) in enumerate(parts):
-            cols = slice(t * P, (t + 1) * P)
-            bank = psum.tile([P, places.stop - places.start], F32, name=f"h2_bank{number}", tag="h_bank0" if number == 0 else f"h2_bank{number}")
-            nc.tensor.matmul_mx(
-                out=bank[:], lhsT=w2_words[:, cols].bitcast(FP8X4), lhsT_scale=w2_plane[:, cols],
-                rhs=xt_words[:, places].bitcast(FP8X4), rhs_scale=xt_plane[:, places], start=True, stop=False,
-            )
+            name = f"h2_bank{number}"
+            bank = psum.tile([P, places.stop - places.start], F32, name=name, tag="h_bank0" if number == 0 else name)
+            product(bank, t, w2_mx, (xt_words, xt_plane), places, True, False)
             h2_parts.append((t, places, bank))
 
-        z_pairs = sb("z_pairs", [P, 2, S, 2], BF16, tag="rounded")
-        for t in (0, 3, 1):
-            nc.vector.tensor_scalar(z_pairs[:, t // 2, :, t % 2], ds[t][:], gain[:, t : t + 1], None, ALU.mult)
-        for c in range(2):
-            cols = slice(c * HALF, (c + 1) * HALF)
-            t = 2
+        z_pairs = sb("z_pairs", [P, 2, S, 2], BF16)
+        z_steps = [(t, slice(0, S)) for t in (0, SCATTERED_BY_VECTOR, 1)] + [(SCATTERED_LAST, cols) for cols in HALVES]
+        for t, cols in z_steps:
             nc.vector.tensor_scalar(z_pairs[:, t // 2, cols, t % 2], ds[t][:, cols], gain[:, t : t + 1], None, ALU.mult)
         z_grouped = sb("z_grouped", [P, PACK * S], BF16)
         z_words = sb("z_words", [P, S], U32)
         z_plane = sb("z_plane", [P, S], U8)
-        pair_words = z_pairs[:].rearrange("p u j e -> p u (j e)").bitcast(F32)
-        for c in range(2):
-            cols = slice(c * HALF, (c + 1) * HALF)
+        pairs = z_pairs[:].rearrange("p u j e -> p u (j e)").bitcast(I32).rearrange("p u j -> p j u")
+        for cols in HALVES:
             nc.vector.tensor_copy(
-                z_grouped[:].bitcast(F32).rearrange("p (j u) -> p j u", u=2)[:, cols, :],
-                pair_words.rearrange("p u j -> p j u")[:, cols, :],
+                z_grouped[:].bitcast(I32).rearrange("p (j u) -> p j u", u=2)[:, cols, :], pairs[:, cols, :]
             )
-        for c in range(2):
-            cols = slice(c * HALF, (c + 1) * HALF)
+        for cols in HALVES:
             nc.vector.quantize_mx(
-                out=z_words[:, cols].bitcast(FP8X4), scales=z_plane[:, cols],
-                in_=z_grouped[:, PACK * c * HALF : PACK * (c + 1) * HALF],
+                out=z_words[:, cols].bitcast(FP8X4),
+                scales=z_plane[:, cols],
+                in_=z_grouped[:, PACK * cols.start : PACK * cols.stop],
             )
         for t, places, bank in h2_parts:
-            cols = slice(t * P, (t + 1) * P)
-            nc.tensor.matmul_mx(
-                out=bank[:], lhsT=w1_words[:, cols].bitcast(FP8X4), lhsT_scale=w1_plane[:, cols],
-                rhs=z_words[:, places].bitcast(FP8X4), rhs_scale=z_plane[:, places], start=False, stop=True,
-            )
+            product(bank, t, w1_mx, (z_words, z_plane), places, False, True)
 
         out_rows = out.rearrange("(p t) j -> t p j", t=PACK)
         value_window = [sb(f"value_window{t}", [P, 2 * S], F32) for t in range(PACK)]
         size_window = [sb(f"size_window{t}", [P, 2 * S], F32) for t in range(PACK)]
-        den = [sb(f"den{t}", [P, S], F32) for t in range(PACK)]
+        size_copy = [value_window[t][:, S:] for t in range(PACK)]
+        size_sum = [sb(f"size_sum{t}", [P, S], F32) for t in range(PACK)]
         for t, places, bank in h2_parts:
             nc.scalar.activation(size_window[t][:, places], bank[:], ACT.Abs)
-        for t in ():
-            nc.scalar.activation(value_window[t][:, S:], h2_parts[t + 1][2][:], ACT.Abs)
-        for t in range(PACK + 1):
-            if t < PACK and t not in ():
-                for part, places, bank in h2_parts:
-                    if part == t:
-                        nc.vector.tensor_copy(value_window[t][:, S:][:, places], size_window[t][:, places])
-            if t > 0:
-                nc.vector.tensor_tensor(den[t - 1][:], size_window[t - 1][:].indirect(n4_list[:]), value_window[t - 1][:, S:], ALU.add)
+        for step in range(PACK + 1):
+            for t, places, bank in h2_parts:
+                if t == step:
+                    nc.vector.tensor_copy(size_copy[t][:, places], size_window[t][:, places])
+            if step > 0:
+                t = step - 1
+                nc.vector.tensor_tensor(size_sum[t][:], size_window[t][:].indirect(n4_list[:]), size_copy[t], ALU.add)
         for t in range(PACK):
-            for part, places, bank in h2_parts:
-                if part == t:
+            for part_tile, places, bank in h2_parts:
+                if part_tile == t:
                     nc.scalar.copy(value_window[t][:, places], bank[:])
-            root = sb(f"root{t}", [P, S], F32)
-            nc.scalar.activation(root[:], den[t][:], ACT.Abs_reciprocal_sqrt, bias=0.5)
+            inverse_root = sb(f"inverse_root{t}", [P, S], F32)
+            nc.scalar.activation(inverse_root[:], size_sum[t][:], ACT.Abs_reciprocal_sqrt, bias=0.5)
+            if t == NUMERATOR_BY_SCALAR:
+                numerator = sb("numerator", [P, S], F32)
+                nc.scalar.activation(numerator[:], value_window[t][:].indirect(n3_list[:]), ACT.Copy)
             inverse = sb(f"inverse{t}", [P, S], F32)
-            nc.scalar.activation(inverse[:], root[:], ACT.Square)
-            pieces = 2 if t == PACK - 1 else 1
-            for c in range(pieces):
-                cols = slice(c * S // pieces, (c + 1) * S // pieces)
-                entries = slice(c * S // pieces // 16, (c + 1) * S // pieces // 16)
-                result = sb(f"result{t}_{c}", [P, S // pieces], F32)
-                nc.vector.tensor_tensor(result[:], value_window[t][:].indirect(n3_list[:, entries]), inverse[:, cols], ALU.mult)
+            nc.scalar.activation(inverse[:], inverse_root[:], ACT.Square)
+            for cols in HALVES if t in STORED_IN_HALVES else [slice(0, S)]:
+                result = sb(f"result{t}_{cols.start}", [P, cols.stop - cols.start], F32)
+                if t == NUMERATOR_BY_SCALAR:
+                    picked = numerator[:, cols]
+                else:
+                    picked = value_window[t][:].indirect(n3_list[:, cols.start // LIST_ROWS : cols.stop // LIST_ROWS])
+                nc.vector.tensor_tensor(result[:], picked, inverse[:, cols], ALU.mult)
                 nc.sync.dma_start(out_rows[t][:, cols], result[:])

from contextlib import ExitStack

import concourse.mybir as mybir

K, T, S, N, G, H, W = 512, 1024, 512, 512, 2048, 512, 384
FLOPS = 2 * K * H * S + 2 * H * N * S + 2 * K * N * S

F32 = mybir.dt.float32
BF16 = mybir.dt.bfloat16
I32 = mybir.dt.int32
U32 = mybir.dt.uint32
U16 = mybir.dt.uint16
U8 = mybir.dt.uint8
FP8X4 = mybir.dt.float8_e4m3fn_x4
ALU = mybir.AluOpType
ACT = mybir.ActivationFunctionType

P = 128
PACK = 4
QUADRANT = 32
BLOCK_PARTITIONS = 8
BLOCKS = K // 32
LIST_ROWS = 16
HALVES = [slice(0, S // 2), slice(S // 2, S)]

H_COPIED_BY_VECTOR = (2, 3)
SCATTERED_BY_VECTOR = 3
SCATTERED_LAST = 2
NUMERATOR_BY_SCALAR = 3
STORED_IN_HALVES = (2, 3)

D_PICKED_AT = 0
XT_PLANE_AT = 0
XT_WORDS_AT = 512
W2_HALVES_AT = (4096, 8192)
D_BYTES_AT = 8192 - 256


def tile_picked_pqmixkminnorm2_none_p_kernel(
    tc, x_words, x_scales, d_words, d_scales, gn, w1, w2, offs, k1, n1, n2, two, n3, n4, out
):
    nc = tc.nc
    with ExitStack() as ctx:
        keep = ctx.enter_context(tc.tile_pool(name="keep", bufs=1))
        shared = ctx.enter_context(tc.tile_pool(name="shared", bufs=1))
        psum = ctx.enter_context(tc.psum_pool(name="psum", bufs=1))

        def sb(name, shape, dtype, tag=None):
            return keep.tile(shape, dtype, name=name, tag=tag or name, align_bytes=64)

        def sb_at(name, shape, dtype, offset):
            return shared.tile(shape, dtype, name=name, offset=offset, align_bytes=64)

        def load_list(name, src):
            tile = sb(name, list(src.shape), U16)
            nc.sync.dma_start(tile[:], src)
            return tile

        def deal(dealt, picked):
            nc.vector.tensor_copy(
                dealt.rearrange("p (t m) -> p m t", t=PACK), picked.rearrange("p (m t) -> p m t", t=PACK)
            )

        def round_weight_half(copy, grouped, cols, raw):
            copy(
                grouped[:].rearrange("p (t m j) -> p m j t", t=PACK, j=PACK)[:, cols.start // PACK : cols.stop // PACK],
                raw.rearrange("p j (m t) -> p m j t", t=PACK),
            )

        def quantise_weight(name, grouped):
            words = sb(name + "_words", [P, N], U32)
            plane = sb(name + "_plane", [P, N], U8)
            nc.vector.quantize_mx(out=words[:].bitcast(FP8X4), scales=plane[:], in_=grouped[:])
            return words, plane

        def product(bank, t, stationary, moving, places, start, stop):
            cols = slice(t * P, (t + 1) * P)
            nc.tensor.matmul_mx(
                out=bank[:],
                lhsT=stationary[0][:, cols].bitcast(FP8X4),
                lhsT_scale=stationary[1][:, cols],
                rhs=moving[0][:, places].bitcast(FP8X4),
                rhs_scale=moving[1][:, places],
                start=start,
                stop=stop,
            )

        x_scale_table = sb("x_scale_table", [P, T], U8)
        d_scale_table = sb("d_scale_table", [P, G], U8)
        x_word_table = sb("x_word_table", [P, T], I32)
        d_word_table = sb("d_word_table", [P, G], I32, tag="dictionary_then_w1")
        d_plane = sb("d_plane", [P, H], U8)
        nc.vector.memset(x_scale_table[:].bitcast(I32), 0)
        nc.vector.memset(d_plane[:].bitcast(I32), 0)
        warm_up = sb("warm_up", [P, 8], F32)
        nc.vector.memset(warm_up[:], 1.0)

        k1_list = load_list("k1_list", k1)
        nc.sync.dma_start(
            d_scale_table[:].bitcast(I32),
            d_scales[0].bitcast(I32).unsqueeze(1).to_broadcast([BLOCKS, BLOCK_PARTITIONS, G // 4]),
        )
        offs_list = load_list("offs_list", offs)
        nc.sync.dma_start(x_word_table[:], x_words[0].rearrange("p n r -> p (n r)").bitcast(I32))
        for j in range(PACK):
            nc.scalar.dma_start(x_scale_table[j::QUADRANT, :].bitcast(I32), x_scales[0, j::PACK, :].bitcast(I32))
        nc.sync.dma_start(d_word_table[:], d_words[0].rearrange("p n r -> p (n r)").bitcast(I32))
        two_list = load_list("two_list", two)
        n2_list = load_list("n2_list", n2)
        n1_list = load_list("n1_list", n1)
        n4_list = load_list("n4_list", n4)
        n3_list = load_list("n3_list", n3)
        gain = sb("gain", [P, PACK], F32)
        nc.sync.dma_start(gain[:], gn.rearrange("(p t) o -> p (t o)", t=PACK))

        nc.scalar.activation(warm_up[:, 0:1], warm_up[:, 1:2], ACT.Abs_reciprocal_sqrt)

        d_bytes = sb_at("d_bytes", [P, H], U8, D_BYTES_AT)
        nc.vector.tensor_copy(d_bytes[:], d_scale_table[:].indirect(k1_list[:]))
        d_bytes_dealt = sb("d_bytes_dealt", [P, H], U8)
        deal(d_bytes_dealt[:], d_bytes[:])
        w2_rows = w2.rearrange("(p j) m -> p j m", j=PACK)
        w2_raw = [sb_at(f"w2_raw{c}", [P, PACK, N // 2], F32, W2_HALVES_AT[c]) for c in range(2)]
        for c, cols in enumerate(HALVES):
            nc.scalar.dma_start(w2_raw[c][:], w2_rows[:, :, cols])
        for j in range(PACK):
            nc.scalar.dma_start(
                d_plane[j::QUADRANT, :].bitcast(I32),
                d_bytes_dealt[BLOCK_PARTITIONS * j :: QUADRANT, :].bitcast(I32),
            )

        xq_plane = sb("xq_plane", [P, S], U8)
        nc.vector.tensor_copy(xq_plane[:], x_scale_table[:].indirect(offs_list[:]))
        xq_words = sb("xq_words", [P, S], U32)
        nc.vector.tensor_copy(xq_words[:], x_word_table[:].bitcast(U32).indirect(offs_list[:]))
        d_picked = sb_at("d_picked", [P, H], U32, D_PICKED_AT)
        nc.vector.tensor_copy(d_picked[:], d_word_table[:].bitcast(U32).indirect(k1_list[:]))
        d_dealt = sb("d_dealt", [P, H], U32)
        deal(d_dealt[:].bitcast(I32), d_picked[:].bitcast(I32))
        w1_raw = sb("w1_raw", [P, PACK, N], F32, tag="dictionary_then_w1")
        nc.sync.dma_start(w1_raw[:], w1.rearrange("(p j) m -> p j m", j=PACK))

        w2_grouped = sb("w2_grouped", [P, PACK * N], BF16)
        for c, cols in enumerate(HALVES):
            round_weight_half(nc.scalar.copy, w2_grouped, cols, w2_raw[c][:])

        h_banks = [psum.tile([P, S], F32, name=f"h_bank{t}") for t in range(PACK)]
        for t in range(PACK):
            product(h_banks[t], t, (d_dealt, d_plane), (xq_words, xq_plane), slice(0, S), True, True)

        ds = [sb(f"ds{t}", [P, 2 * S if t == SCATTERED_BY_VECTOR else S], F32) for t in range(PACK)]
        minus_half_pa = [sb(f"minus_half_pa{t}", [P, W], F32) for t in range(PACK)]
        for t in range(PACK):
            if t in H_COPIED_BY_VECTOR:
                nc.vector.tensor_scalar(ds[t][:, :S], h_banks[t][:], 0.0625, None, ALU.mult)
            else:
                nc.scalar.activation(ds[t][:, :S], h_banks[t][:], ACT.Copy, scale=0.0625)
            nc.scalar.activation(minus_half_pa[t][:], ds[t][:].indirect(n2_list[:]), ACT.Copy, scale=-0.5)
        smaller = [sb(f"smaller{t}", [P, W], F32) for t in range(PACK)]
        for t in range(PACK):
            if t == SCATTERED_BY_VECTOR:
                old = sb("old", [P, W], F32)
                nc.scalar.activation(old[:], ds[t][:].indirect(n1_list[:]), ACT.Copy)
                nc.vector.scalar_tensor_tensor(smaller[t][:], minus_half_pa[t][:], -2.0, old[:], ALU.mult, ALU.min)
            else:
                old_less = sb(f"old_less{t}", [P, W], F32)
                nc.vector.tensor_tensor(old_less[:], ds[t][:].indirect(n1_list[:]), minus_half_pa[t][:], ALU.add)
                nc.vector.scalar_tensor_tensor(smaller[t][:], minus_half_pa[t][:], -1.0, old_less[:], ALU.mult, ALU.min)
        for t in range(PACK):
            if t == SCATTERED_BY_VECTOR:
                nc.vector.tensor_tensor(ds[t][:].indirect(n1_list[:]), smaller[t][:], minus_half_pa[t][:], ALU.add)
            else:
                nc.scalar.activation(ds[t][:].indirect(n1_list[:]), smaller[t][:], ACT.Copy)

        xt_words = sb_at("xt_words", [P, S], U32, XT_WORDS_AT)
        nc.vector.tensor_copy(xt_words[:], x_word_table[:].bitcast(U32).indirect(two_list[:]))
        xt_plane = sb_at("xt_plane", [P, S], U8, XT_PLANE_AT)
        nc.vector.tensor_copy(xt_plane[:], x_scale_table[:].indirect(two_list[:]))

        w2_mx = quantise_weight("w2", w2_grouped)
        w1_grouped = sb("w1_grouped", [P, PACK * N], BF16)
        for cols in HALVES:
            round_weight_half(nc.vector.tensor_copy, w1_grouped, cols, w1_raw[:, :, cols])
        w1_mx = quantise_weight("w1", w1_grouped)

        parts = [(0, places) for places in HALVES] + [(t, slice(0, S)) for t in range(1, PACK)]
        h2_parts = []
        for number, (t, places) in enumerate(parts):
            name = f"h2_bank{number}"
            bank = psum.tile([P, places.stop - places.start], F32, name=name, tag="h_bank0" if number == 0 else name)
            product(bank, t, w2_mx, (xt_words, xt_plane), places, True, False)
            h2_parts.append((t, places, bank))

        z_pairs = sb("z_pairs", [P, 2, S, 2], BF16)
        z_steps = [(t, slice(0, S)) for t in (0, SCATTERED_BY_VECTOR, 1)] + [(SCATTERED_LAST, cols) for cols in HALVES]
        for t, cols in z_steps:
            nc.vector.tensor_scalar(z_pairs[:, t // 2, cols, t % 2], ds[t][:, cols], gain[:, t : t + 1], None, ALU.mult)
        z_grouped = sb("z_grouped", [P, PACK * S], BF16)
        z_words = sb("z_words", [P, S], U32)
        z_plane = sb("z_plane", [P, S], U8)
        pairs = z_pairs[:].rearrange("p u j e -> p u (j e)").bitcast(I32).rearrange("p u j -> p j u")
        for cols in HALVES:
            nc.vector.tensor_copy(
                z_grouped[:].bitcast(I32).rearrange("p (j u) -> p j u", u=2)[:, cols, :], pairs[:, cols, :]
            )
        for cols in HALVES:
            nc.vector.quantize_mx(
                out=z_words[:, cols].bitcast(FP8X4),
                scales=z_plane[:, cols],
                in_=z_grouped[:, PACK * cols.start : PACK * cols.stop],
            )
        for t, places, bank in h2_parts:
            product(bank, t, w1_mx, (z_words, z_plane), places, False, True)

        out_rows = out.rearrange("(p t) j -> t p j", t=PACK)
        value_window = [sb(f"value_window{t}", [P, 2 * S], F32) for t in range(PACK)]
        size_window = [sb(f"size_window{t}", [P, 2 * S], F32) for t in range(PACK)]
        size_copy = [value_window[t][:, S:] for t in range(PACK)]
        size_sum = [sb(f"size_sum{t}", [P, S], F32) for t in range(PACK)]
        for t, places, bank in h2_parts:
            nc.scalar.activation(size_window[t][:, places], bank[:], ACT.Abs)
        for step in range(PACK + 1):
            for t, places, bank in h2_parts:
                if t == step:
                    nc.vector.tensor_copy(size_copy[t][:, places], size_window[t][:, places])
            if step > 0:
                t = step - 1
                nc.vector.tensor_tensor(size_sum[t][:], size_window[t][:].indirect(n4_list[:]), size_copy[t], ALU.add)
        for t in range(PACK):
            for part_tile, places, bank in h2_parts:
                if part_tile == t:
                    nc.scalar.copy(value_window[t][:, places], bank[:])
            inverse_root = sb(f"inverse_root{t}", [P, S], F32)
            nc.scalar.activation(inverse_root[:], size_sum[t][:], ACT.Abs_reciprocal_sqrt, bias=0.5)
            if t == NUMERATOR_BY_SCALAR:
                numerator = sb("numerator", [P, S], F32)
                nc.scalar.activation(numerator[:], value_window[t][:].indirect(n3_list[:]), ACT.Copy)
            inverse = sb(f"inverse{t}", [P, S], F32)
            nc.scalar.activation(inverse[:], inverse_root[:], ACT.Square)
            for cols in HALVES if t in STORED_IN_HALVES else [slice(0, S)]:
                result = sb(f"result{t}_{cols.start}", [P, cols.stop - cols.start], F32)
                if t == NUMERATOR_BY_SCALAR:
                    picked = numerator[:, cols]
                else:
                    picked = value_window[t][:].indirect(n3_list[:, cols.start // LIST_ROWS : cols.stop // LIST_ROWS])
                nc.vector.tensor_tensor(result[:], picked, inverse[:, cols], ALU.mult)
                nc.sync.dma_start(out_rows[t][:, cols], result[:])
